import numpy as np
import ml_dtypes

BF16 = ml_dtypes.bfloat16


def bf(x):
    return np.asarray(x, np.float32).astype(BF16)


def f32(x):
    return np.asarray(x, np.float32)


def f64(x):
    return np.asarray(x).astype(np.float64)


def striped(idx):
    return np.tile(idx.reshape(-1, 16).T, (8, 1))


S, K, M, N, B, Q = 512, 256, 128, 128, 2, 64


def setup_inputs():
    return {"base": bf(np.random.standard_normal((B, M, S))), "x": bf(np.random.standard_normal((K, N))), "w": bf(np.random.standard_normal((K, M)) / np.sqrt(K)), "offs": striped(np.random.permutation(S)[:N])}


def reference(base, x, w, offs):
    idx = offs[:16].T.reshape(-1)
    z = f64(base).copy()
    for i in range(B):
        z[i][:, idx[i * Q : (i + 1) * Q]] += f64(w).T @ f64(x)[:, i * Q : (i + 1) * Q]
    return z

@@ -1,0 +1,55 @@
+import concourse.mybir as mybir
+from concourse.masks import make_identity
+
+BF16, F32, U16 = mybir.dt.bfloat16, mybir.dt.float32, mybir.dt.uint16
+
+P = 128
+B = 2
+S = 512
+K = 256
+KB = K // P
+N = 128
+Q = N // B
+QC = Q // 16
+
+FLOPS = 2 * K * P * N
+
+
+def tile_scatter_matmul_kernel(tc, base, x, w, offs, out):
+    nc = tc.nc
+    with (
+        tc.tile_pool(name="held", bufs=1) as held,
+        tc.psum_pool(name="banks", bufs=1) as banks,
+    ):
+        offsets = held.tile([P, N // 16], U16, name="offsets")
+        nc.sync.dma_start(offsets[:], offs)
+        base_tiles = [held.tile([P, S], BF16, name=f"base{i}") for i in range(B)]
+        nc.sync.dma_start(base_tiles[0][:], base[0])
+        nc.scalar.dma_start(base_tiles[1][:], base[1])
+        w_tile = held.tile([P, KB, P], BF16, name="w_tile")
+        nc.scalar.dma_start(w_tile[:], w.rearrange("(kb p) m -> p kb m", p=P))
+        x_tile = held.tile([P, KB, N], BF16, name="x_tile")
+        nc.sync.dma_start(x_tile[:], x.rearrange("(kb p) n -> p kb n", p=P))
+
+        identity = held.tile([P, P], BF16, name="identity")
+        make_identity(nc, identity[:])
+
+        windows = [banks.tile([P, S], F32, name=f"window{i}") for i in range(B)]
+        for i in range(B):
+            nc.tensor.matmul(windows[i][:], identity[:], base_tiles[i][:], start=True, stop=False)
+
+        for i in range(B):
+            places = windows[i][:].indirect(offsets[:, i * QC : (i + 1) * QC])
+            for kb in range(KB):
+                nc.tensor.matmul(
+                    places,
+                    w_tile[:, kb, :],
+                    x_tile[:, kb, i * Q : (i + 1) * Q],
+                    start=False,
+                    stop=(kb == KB - 1),
+                )
+
+        for i in range(B):
+            staged = held.tile([P, S], F32, name=f"staged{i}")
+            nc.vector.tensor_copy(staged[:], windows[i][:])
+            nc.sync.dma_start(out[i], staged[:])

@@ -49,7 +49,8 @@ def tile_scatter_matmul_kernel(tc, base, x, w, offs, out):
                     stop=(kb == KB - 1),
                 )
 
-        for i in range(B):
-            staged = held.tile([P, S], F32, name=f"staged{i}")
-            nc.vector.tensor_copy(staged[:], windows[i][:])
-            nc.sync.dma_start(out[i], staged[:])
+        staged = [held.tile([P, S], F32, name=f"staged{i}") for i in range(B)]
+        nc.scalar.copy(staged[0][:], windows[0][:])
+        nc.scalar.dma_start(out[0], staged[0][:])
+        nc.vector.tensor_copy(staged[1][:], windows[1][:])
+        nc.sync.dma_start(out[1], staged[1][:])

@@ -12,6 +12,8 @@ N = 128
 Q = N // B
 QC = Q // 16
 
+WARM = 16
+
 FLOPS = 2 * K * P * N
 
 
@@ -30,6 +32,12 @@ def tile_scatter_matmul_kernel(tc, base, x, w, offs, out):
         nc.scalar.dma_start(w_tile[:], w.rearrange("(kb p) m -> p kb m", p=P))
         x_tile = held.tile([P, KB, N], BF16, name="x_tile")
         nc.sync.dma_start(x_tile[:], x.rearrange("(kb p) n -> p kb n", p=P))
+
+        zeros = held.tile([P, P], BF16, name="zeros")
+        nc.gpsimd.memset(zeros[:], 0.0)
+        idle_bank = banks.tile([P, P], F32, name="idle_bank")
+        for step in range(WARM):
+            nc.tensor.matmul(idle_bank[:], zeros[:], zeros[:], start=True, stop=True)
 
         identity = held.tile([P, P], BF16, name="identity")
         make_identity(nc, identity[:])

@@ -23,15 +23,15 @@ def tile_scatter_matmul_kernel(tc, base, x, w, offs, out):
         tc.tile_pool(name="held", bufs=1) as held,
         tc.psum_pool(name="banks", bufs=1) as banks,
     ):
+        base_tiles = [held.tile([P, S], BF16, name=f"base{i}") for i in range(B)]
+        for i in range(B):
+            nc.sync.dma_start(base_tiles[i][:], base[i])
+        w_tile = held.tile([P, KB, P], BF16, name="w_tile")
+        nc.sync.dma_start(w_tile[:], w.rearrange("(p kb) m -> p kb m", kb=KB))
+        x_tile = held.tile([P, KB, N], BF16, name="x_tile")
+        nc.sync.dma_start(x_tile[:], x.rearrange("(p kb) n -> p kb n", kb=KB))
         offsets = held.tile([P, N // 16], U16, name="offsets")
         nc.sync.dma_start(offsets[:], offs)
-        base_tiles = [held.tile([P, S], BF16, name=f"base{i}") for i in range(B)]
-        nc.sync.dma_start(base_tiles[0][:], base[0])
-        nc.scalar.dma_start(base_tiles[1][:], base[1])
-        w_tile = held.tile([P, KB, P], BF16, name="w_tile")
-        nc.scalar.dma_start(w_tile[:], w.rearrange("(kb p) m -> p kb m", p=P))
-        x_tile = held.tile([P, KB, N], BF16, name="x_tile")
-        nc.sync.dma_start(x_tile[:], x.rearrange("(kb p) n -> p kb n", p=P))
 
         zeros = held.tile([P, P], BF16, name="zeros")
         nc.gpsimd.memset(zeros[:], 0.0)

@@ -12,7 +12,7 @@ N = 128
 Q = N // B
 QC = Q // 16
 
-WARM = 16
+WARM = 12
 
 FLOPS = 2 * K * P * N
 

@@ -12,7 +12,7 @@ N = 128
 Q = N // B
 QC = Q // 16
 
-WARM = 12
+WARM = 10
 
 FLOPS = 2 * K * P * N
 

@@ -58,7 +58,7 @@ def tile_scatter_matmul_kernel(tc, base, x, w, offs, out):
                 )
 
         staged = [held.tile([P, S], F32, name=f"staged{i}") for i in range(B)]
-        nc.scalar.copy(staged[0][:], windows[0][:])
-        nc.scalar.dma_start(out[0], staged[0][:])
-        nc.vector.tensor_copy(staged[1][:], windows[1][:])
-        nc.sync.dma_start(out[1], staged[1][:])
+        nc.vector.tensor_copy(staged[0][:], windows[0][:])
+        nc.sync.dma_start(out[0], staged[0][:])
+        nc.scalar.copy(staged[1][:], windows[1][:])
+        nc.scalar.dma_start(out[1], staged[1][:])

@@ -33,11 +33,12 @@ def tile_scatter_matmul_kernel(tc, base, x, w, offs, out):
         offsets = held.tile([P, N // 16], U16, name="offsets")
         nc.sync.dma_start(offsets[:], offs)
 
-        zeros = held.tile([P, P], BF16, name="zeros")
+        zeros = held.tile([P, 2], BF16, name="zeros")
         nc.gpsimd.memset(zeros[:], 0.0)
+        zero_block = zeros[:, 0:1].to_broadcast([P, P])
         idle_bank = banks.tile([P, P], F32, name="idle_bank")
         for step in range(WARM):
-            nc.tensor.matmul(idle_bank[:], zeros[:], zeros[:], start=True, stop=True)
+            nc.tensor.matmul(idle_bank[:], zero_block, zero_block, start=True, stop=True)
 
         identity = held.tile([P, P], BF16, name="identity")
         make_identity(nc, identity[:])

@@ -27,9 +27,9 @@ def tile_scatter_matmul_kernel(tc, base, x, w, offs, out):
         for i in range(B):
             nc.sync.dma_start(base_tiles[i][:], base[i])
         w_tile = held.tile([P, KB, P], BF16, name="w_tile")
-        nc.sync.dma_start(w_tile[:], w.rearrange("(p kb) m -> p kb m", kb=KB))
+        nc.scalar.dma_start(w_tile[:], w.rearrange("(p kb) m -> p kb m", kb=KB))
         x_tile = held.tile([P, KB, N], BF16, name="x_tile")
-        nc.sync.dma_start(x_tile[:], x.rearrange("(p kb) n -> p kb n", kb=KB))
+        nc.scalar.dma_start(x_tile[:], x.rearrange("(p kb) n -> p kb n", kb=KB))
         offsets = held.tile([P, N // 16], U16, name="offsets")
         nc.sync.dma_start(offsets[:], offs)
 

import concourse.mybir as mybir
from concourse.masks import make_identity

BF16, F32, U16 = mybir.dt.bfloat16, mybir.dt.float32, mybir.dt.uint16

P = 128
B = 2
S = 512
K = 256
KB = K // P
N = 128
Q = N // B
QC = Q // 16

WARM = 10

FLOPS = 2 * K * P * N


def tile_scatter_matmul_kernel(tc, base, x, w, offs, out):
    nc = tc.nc
    with (
        tc.tile_pool(name="held", bufs=1) as held,
        tc.psum_pool(name="banks", bufs=1) as banks,
    ):
        base_tiles = [held.tile([P, S], BF16, name=f"base{i}") for i in range(B)]
        for i in range(B):
            nc.sync.dma_start(base_tiles[i][:], base[i])
        w_tile = held.tile([P, KB, P], BF16, name="w_tile")
        nc.scalar.dma_start(w_tile[:], w.rearrange("(p kb) m -> p kb m", kb=KB))
        x_tile = held.tile([P, KB, N], BF16, name="x_tile")
        nc.scalar.dma_start(x_tile[:], x.rearrange("(p kb) n -> p kb n", kb=KB))
        offsets = held.tile([P, N // 16], U16, name="offsets")
        nc.sync.dma_start(offsets[:], offs)

        zeros = held.tile([P, 2], BF16, name="zeros")
        nc.gpsimd.memset(zeros[:], 0.0)
        zero_block = zeros[:, 0:1].to_broadcast([P, P])
        idle_bank = banks.tile([P, P], F32, name="idle_bank")
        for step in range(WARM):
            nc.tensor.matmul(idle_bank[:], zero_block, zero_block, start=True, stop=True)

        identity = held.tile([P, P], BF16, name="identity")
        make_identity(nc, identity[:])

        windows = [banks.tile([P, S], F32, name=f"window{i}") for i in range(B)]
        for i in range(B):
            nc.tensor.matmul(windows[i][:], identity[:], base_tiles[i][:], start=True, stop=False)

        for i in range(B):
            places = windows[i][:].indirect(offsets[:, i * QC : (i + 1) * QC])
            for kb in range(KB):
                nc.tensor.matmul(
                    places,
                    w_tile[:, kb, :],
                    x_tile[:, kb, i * Q : (i + 1) * Q],
                    start=False,
                    stop=(kb == KB - 1),
                )

        staged = [held.tile([P, S], F32, name=f"staged{i}") for i in range(B)]
        nc.vector.tensor_copy(staged[0][:], windows[0][:])
        nc.sync.dma_start(out[0], staged[0][:])
        nc.scalar.copy(staged[1][:], windows[1][:])
        nc.scalar.dma_start(out[1], staged[1][:])
